import numpy as np
import ml_dtypes


def mxq(x, axis, fmt="e4m3"):
    dtype, down = {"e4m3": (ml_dtypes.float8_e4m3fn, 7), "e5m2": (ml_dtypes.float8_e5m2, 14)}[fmt]
    v = np.moveaxis(np.asarray(x, np.float32).astype(ml_dtypes.bfloat16).astype(np.float64), axis, -1)
    blocks = v.reshape(v.shape[:-1] + (-1, 32))
    amax = np.abs(blocks).max(-1, keepdims=True)
    byte = np.maximum(np.where(amax > 0, np.frexp(amax)[1] - 1 + 127, 0) - down, 1)
    scale = np.exp2(byte - 127.0)
    codes = (blocks / scale).astype(np.float32).astype(dtype).astype(np.float64)
    return np.moveaxis((codes * scale).reshape(v.shape), -1, axis)


WIDE = False


def mx_kscale(k):
    if not WIDE:
        return np.ones(k)
    levels = np.array([30, -30])
    if k % 512:
        return np.exp2(np.random.permutation(np.resize(levels, k // 32))).repeat(32)
    a = np.empty((k // 512, 16))
    for p in range(k // 512):
        a[p, :8] = np.random.permutation(np.resize(levels, 8))
        for g in range(8):
            far = levels[np.abs(levels - a[p, g]) >= 10]
            a[p, g + 8] = far[np.random.randint(len(far))]
    return np.exp2(a.ravel()).repeat(32)


BF16 = ml_dtypes.bfloat16


def bf(x):
    return np.asarray(x, np.float32).astype(BF16)


def f64(x):
    return np.asarray(x).astype(np.float64)


E2M1 = np.array([0.0, 0.5, 1.0, 1.5, 2.0, 3.0, 4.0, 6.0, -0.0, -0.5, -1.0, -1.5, -2.0, -3.0, -4.0, -6.0])


def pack_weight(w, fmt):
    k, n = w.shape
    w = f64(bf(w)).reshape(k // 32, 32, n)
    amax = np.abs(w).max(1)
    if fmt in ("e4m3", "e5m2"):
        byte = np.frexp(amax)[1] - 1 + 127 - (7 if fmt == "e4m3" else 14)
    else:
        mant, ex = np.frexp(amax / 6.0)
        byte = np.where(mant > 0.5, ex, ex - 1) + 127
    byte = np.clip(np.where(amax > 0, byte, 1), 1, 254)
    scaled = (w * np.exp2(127.0 - byte)[:, None, :]).reshape(k, n).astype(np.float32)
    by_word = np.ascontiguousarray(scaled.reshape(k // 512, 128, 4, n).transpose(0, 1, 3, 2))
    if fmt in ("e4m3", "e5m2"):
        words = by_word.astype(ml_dtypes.float8_e4m3fn if fmt == "e4m3" else ml_dtypes.float8_e5m2).view(np.uint8)
    else:
        c = by_word.astype(ml_dtypes.float4_e2m1fn).view(np.uint8) & 0xF
        words = c[..., 0::2] | (c[..., 1::2] << 4)
    return np.ascontiguousarray(words), np.ascontiguousarray(byte.astype(np.uint8).reshape(k // 512, 16, n))


def unpack_weight(words, scales, fmt):
    g, p, n, _ = words.shape
    if fmt in ("e4m3", "e5m2"):
        vals = np.ascontiguousarray(words).view(ml_dtypes.float8_e4m3fn if fmt == "e4m3" else ml_dtypes.float8_e5m2).astype(np.float64)
    else:
        nib = np.empty((g, p, n, 4), np.uint8)
        nib[..., 0::2] = words & 0xF
        nib[..., 1::2] = words >> 4
        vals = E2M1[nib]
    vals = vals * np.repeat(np.exp2(scales.astype(np.float64) - 127.0), 8, axis=1)[..., None]
    return vals.transpose(0, 1, 3, 2).reshape(g * 512, n)


T, D, F = 1024, 1024, 2048


def setup_inputs():
    s, t = mx_kscale(D), mx_kscale(F)
    G = np.random.standard_normal((D, T)) * np.exp(0.5 * np.random.standard_normal((D, T)))
    u_words, u_scales = pack_weight(G * s[:, None], "e5m2")
    return {"u_words": u_words, "u_scales": u_scales,
            "w_out": bf(np.random.standard_normal((D, F)) / np.sqrt(D) / s[:, None] * t),
            "act": bf(np.tanh(0.8 * np.random.standard_normal((T, F)))),
            "w_in": bf(np.random.standard_normal((F, D)) / np.sqrt(F) / t[:, None]),
            "loss_grad": bf(0.5 * np.random.standard_normal((T, D)))}


def reference(u_words, u_scales, w_out, act, w_in, loss_grad):
    u = unpack_weight(u_words, u_scales, "e5m2")
    back = u.T @ mxq(f64(w_out), 0, "e4m3")
    pre = back * (1.0 - np.square(f64(act)))
    vjp = mxq(pre, 1, "e5m2") @ mxq(f64(w_in), 0, "e4m3")
    return vjp + f64(loss_grad)

@@ -1,0 +1,288 @@
+from contextlib import ExitStack
+import concourse.mybir as mybir
+from concourse.masks import make_identity
+F32 = mybir.dt.float32
+BF16 = mybir.dt.bfloat16
+U32 = mybir.dt.uint32
+I32 = mybir.dt.int32
+U8 = mybir.dt.uint8
+E4X4 = mybir.dt.float8_e4m3fn_x4
+E5X4 = mybir.dt.float8_e5m2_x4
+ALU = mybir.AluOpType
+ACT = mybir.ActivationFunctionType
+T, D, F = 1024, 1024, 2048
+FLOPS = 2 * 2 * T * D * F
+P = 128
+N = 512
+NT = T // P
+NC = F // N
+NG = D // N
+NH = D // N
+PLAN = {"wo": [("vv", "ss")] * 3, "wi": {}}
+N1 = 4
+
+def tile_implicit_adjoint_step_e3_kernel(tc, u_words, u_scales, w_out, act, w_in, loss_grad, out):
+    nc = tc.nc
+    with ExitStack() as ctx:
+        keep = ctx.enter_context(tc.tile_pool(name="keep", bufs=1))
+        raws = ctx.enter_context(tc.tile_pool(name="raws", bufs=8))
+        work = ctx.enter_context(tc.tile_pool(name="work", bufs=4))
+        psum = ctx.enter_context(tc.psum_pool(name="psum", bufs=8))
+
+        u_c = keep.tile([P, NG, T], U32, name="u_c", align_bytes=64)
+        u_s = keep.tile([P, NG, T], U8, name="u_s", align_bytes=64)
+        wo_c = keep.tile([P, NC, NG, N], U32, name="wo_c", align_bytes=64)
+        wo_s = keep.tile([P, NC, NG, N], U8, name="wo_s", align_bytes=64)
+        wi_c = keep.tile([P, NH, NC, N], U32, name="wi_c", align_bytes=64)
+        wi_s = keep.tile([P, NH, NC, N], U8, name="wi_s", align_bytes=64)
+        pa_c = keep.tile([P, NC, N1 * P], U32, name="pa_c", align_bytes=64)
+        pa_s = keep.tile([P, NC, N1 * P], U8, name="pa_s", align_bytes=64)
+        pb_c = keep.tile([P, NT - N1, NC, P], U32, name="pb_c", align_bytes=64)
+        pb_s = keep.tile([P, NT - N1, NC, P], U8, name="pb_s", align_bytes=64)
+        ident = keep.tile([P, P], F32, name="ident", align_bytes=64)
+
+        nc.gpsimd.memset(u_s[:].rearrange("p g n -> p (g n)").bitcast(I32), 0)
+        make_identity(nc, ident[:])
+
+        wo_v = w_out.rearrange("(g p j) f -> g p j f", p=P, j=4)
+        wi_v = w_in.rearrange("(c p j) d -> c p j d", p=P, j=4)
+        act_v = act.rearrange("(i p) f -> p i f", p=P)
+        lg_v = loss_grad.rearrange("(i p) d -> i p d", p=P)
+        out_v = out.rearrange("(i p) d -> i p d", p=P)
+
+        wo_raw, act1, act2, wi_raw, lg = {}, {}, {}, {}, {}
+
+        def load_wo(c, g):
+            t = raws.tile([P, 4, N], BF16, name="raw", bufs=12, align_bytes=64)
+            nc.sync.dma_start(out=t[:], in_=wo_v[g, :, :, c * N:(c + 1) * N])
+            wo_raw[c, g] = t
+
+        def load_act1(c):
+            t = raws.tile([P, N1, N], BF16, name="act1", bufs=4)
+            nc.sync.dma_start(out=t[:], in_=act_v[:, 0:N1, c * N:(c + 1) * N])
+            act1[c] = t
+
+        def load_act2(i):
+            t = raws.tile([P, F], BF16, name="act2", bufs=4)
+            nc.sync.dma_start(out=t[:], in_=act_v[:, i, :])
+            act2[i] = t
+
+        def load_wi(c, h):
+            t = raws.tile([P, 4, N], BF16, name="raw", bufs=12, align_bytes=64)
+            nc.sync.dma_start(out=t[:], in_=wi_v[c, :, :, h * N:(h + 1) * N])
+            wi_raw[c, h] = t
+
+        def load_lg(i):
+            t = raws.tile([P, D], BF16, name="lg", bufs=8)
+            nc.sync.dma_start(out=t[:], in_=lg_v[i])
+            lg[i] = t
+
+        grouped = {}
+
+        def spread_wo(c, g, engs):
+            raw = wo_raw[c, g]
+            if ("o", c, g) not in grouped:
+                grouped["o", c, g] = work.tile([P, N, 4], BF16, name="grouped", bufs=5, align_bytes=64)
+            dst = grouped["o", c, g]
+            for u, e in enumerate(engs):
+                o = dst[:, u * 256:(u + 1) * 256, :].rearrange("p (q e) t -> p q t e", e=2)
+                s = raw[:].rearrange("p t (q u e) -> p u q t e", u=2, e=2)[:, u]
+                if e == "v":
+                    nc.vector.tensor_copy(out=o, in_=s)
+                elif e == "s":
+                    nc.scalar.copy(out=o, in_=s)
+                elif e == "g":
+                    nc.gpsimd.tensor_scalar(out=dst[:, u * 256:(u + 1) * 256, :].rearrange("p (q e) t -> p q e t", e=2), in0=raw[:].rearrange("p t (q u e) -> p u q e t", u=2, e=2)[:, u], scalar1=1.0, scalar2=0.0, op0=ALU.mult, op1=ALU.add)
+
+        def spread(raw, key, parts):
+            if key not in grouped:
+                grouped[key] = work.tile([P, N, 4], BF16, name="grouped", bufs=5, align_bytes=64)
+            dst = grouped[key]
+            for e, a, b in parts:
+                o = dst[:, a:b, :].rearrange("p (c i) t -> p c t i", i=4)
+                s = raw[:, :, a:b].rearrange("p t (c i) -> p c t i", i=4)
+                if e == "v":
+                    nc.vector.tensor_copy(out=o, in_=s)
+                elif e == "s":
+                    nc.scalar.copy(out=o, in_=s)
+                else:
+                    nc.gpsimd.tensor_scalar(out=dst[:, a:b, :], in0=raw[:, :, a:b].rearrange("p t c -> p c t"), scalar1=1.0, scalar2=0.0, op0=ALU.mult, op1=ALU.add)
+
+        def quant_wo(c, g):
+            nc.vector.quantize_mx(out=wo_c[:, c, g, :].bitcast(E4X4), scales=wo_s[:, c, g, :], in_=grouped.pop(("o", c, g))[:].rearrange("p c t -> p (c t)"))
+
+        def quant_wi(c, h):
+            nc.vector.quantize_mx(out=wi_c[:, h, c, :].bitcast(E4X4), scales=wi_s[:, h, c, :], in_=grouped.pop(("i", c, h))[:].rearrange("p c t -> p (c t)"))
+
+        def spread_wi(c, h, parts):
+            spread(wi_raw[c, h], ("i", c, h), parts)
+
+        back, sq, pre, turned, gpre = {}, {}, {}, {}, {}
+
+        def stage1(c, i, gs=(0, 1)):
+            if (c, i) not in back:
+                back[c, i] = psum.tile([P, N], F32, name="bank")
+            for g in gs:
+                nc.tensor.matmul_mx(out=back[c, i][:], lhsT=u_c[:, g, i * P:(i + 1) * P].bitcast(E5X4), lhsT_scale=u_s[:, g, i * P:(i + 1) * P],
+                                    rhs=wo_c[:, c, g, :].bitcast(E4X4), rhs_scale=wo_s[:, c, g, :], start=(g == 0), stop=(g == NG - 1))
+
+        def square(c, i):
+            t = work.tile([P, N], F32, name="sq", bufs=8)
+            src = act1[c][:, i, :] if i < N1 else act2[i][:, c * N:(c + 1) * N]
+            nc.scalar.activation(out=t[:].rearrange("q (u p e) -> q u p e", u=2, e=2), in_=src.rearrange("q (p u e) -> q u p e", u=2, e=2), func=ACT.Square)
+            sq[c, i] = t
+
+        def gate(c, i):
+            t = work.tile([P, N], BF16, name="pre", bufs=8)
+            nc.vector.scalar_tensor_tensor(out=t[:], in0=sq.pop((c, i))[:], scalar=1.0, in1=back.pop((c, i))[:], op0=ALU.subtract, op1=ALU.mult)
+            pre[c, i] = t
+
+        def turn(pairs):
+            t = psum.tile([P, 2, 2, P], F32, name="bank")
+            for k, ci in enumerate(pairs):
+                w = pre.pop(ci)[:].bitcast(F32)
+                for u in (0, 1):
+                    nc.tensor.transpose(out=t[:, k, u, :], in_=w[:, u * P:(u + 1) * P], identity=ident[:])
+            turned[pairs[0]] = t
+
+        def empty(pairs, key, slot, eng):
+            if key not in gpre:
+                gpre[key] = work.tile([P, 4 * P, 4], BF16, name="gpre", bufs=3, align_bytes=64)
+            dst = gpre[key][:, slot * 256:(slot + 1) * 256, :].rearrange("p r t -> p (r t)").bitcast(F32).rearrange("p (k r u) -> p k r u", k=2, u=2)
+            src = turned.pop(pairs[0])[:].rearrange("p k u r -> p k r u")
+            if eng == "s":
+                nc.scalar.copy(out=dst, in_=src)
+            else:
+                nc.vector.tensor_copy(out=dst, in_=src)
+
+        def quant_pa(c):
+            nc.vector.quantize_mx(out=pa_c[:, c, :].bitcast(E5X4), scales=pa_s[:, c, :], in_=gpre.pop(("a", c))[:].rearrange("p r t -> p (r t)"))
+
+        def quant_pb(i):
+            nc.vector.quantize_mx(out=pb_c[:, i - N1].rearrange("p c r -> p (c r)").bitcast(E5X4), scales=pb_s[:, i - N1].rearrange("p c r -> p (c r)"), in_=gpre.pop(("b", i))[:].rearrange("p r t -> p (r t)"))
+
+        vjp = {}
+
+        def stage2(i, h):
+            t = psum.tile([P, N], F32, name="bank")
+            for c in range(NC):
+                if i < N1:
+                    l, s = pa_c[:, c, i * P:(i + 1) * P], pa_s[:, c, i * P:(i + 1) * P]
+                else:
+                    l, s = pb_c[:, i - N1, c, :], pb_s[:, i - N1, c, :]
+                nc.tensor.matmul_mx(out=t[:], lhsT=l.bitcast(E5X4), lhsT_scale=s, rhs=wi_c[:, h, c, :].bitcast(E4X4), rhs_scale=wi_s[:, h, c, :], start=(c == 0), stop=(c == NC - 1))
+            vjp[i, h] = t
+
+        def finish(i, h):
+            t = work.tile([P, N], F32, name="res", bufs=4)
+            nc.vector.tensor_tensor(out=t[:], in0=lg[i][:, h * N:(h + 1) * N], in1=vjp.pop((i, h))[:], op=ALU.subtract)
+            nc.sync.dma_start(out=out_v[i, :, h * N:(h + 1) * N], in_=t[:])
+
+        uw = u_words.rearrange("g p n t -> p g (n t)")
+        def load_u(g):
+            nc.sync.dma_start(out=u_c[:, g, :].bitcast(I32), in_=uw[:, g, :].bitcast(I32))
+        load_wo(0, 0)
+        load_wo(0, 1)
+        for q in range(4):
+            nc.sync.dma_start(out=u_s[32 * q:32 * q + 4, :, :].bitcast(I32), in_=u_scales[:, 4 * q:4 * q + 4, :].rearrange("g q n -> q g n").bitcast(I32))
+        load_u(0)
+        load_act1(0)
+        load_u(1)
+        for c in range(1, NC):
+            load_wo(c, 0)
+            load_wo(c, 1)
+            load_act1(c)
+        load_wi(0, 0)
+        load_act2(4)
+        load_wi(1, 0)
+        load_wi(2, 0)
+        load_act2(5)
+        load_wi(3, 0)
+        load_act2(6)
+        load_act2(7)
+
+        W = [("v", 0, N)]
+        spread_wo(0, 0, "vs")
+        spread_wo(0, 1, "vs")
+        quant_wo(0, 0)
+        quant_wo(0, 1)
+        for i in range(N1):
+            stage1(0, i, (0,))
+        for i in range(N1):
+            stage1(0, i, (1,))
+        for i in range(N1):
+            square(0, i)
+        for c in range(NC):
+            if c + 1 < NC:
+                spread_wo(c + 1, 0, PLAN["wo"][c][0])
+                spread_wo(c + 1, 1, PLAN["wo"][c][1])
+                quant_wo(c + 1, 0)
+            else:
+                spread_wi(0, 0, [("g", 0, N)])
+                spread_wi(1, 0, [("g", 0, N)])
+            gate(c, 0)
+            gate(c, 1)
+            turn([(c, 0), (c, 1)])
+            empty([(c, 0), (c, 1)], ("a", c), 0, "s")
+            gate(c, 2)
+            gate(c, 3)
+            turn([(c, 2), (c, 3)])
+            empty([(c, 2), (c, 3)], ("a", c), 1, "s")
+            if c + 1 < NC:
+                quant_wo(c + 1, 1)
+                for i in range(N1):
+                    stage1(c + 1, i)
+                for i in range(N1):
+                    square(c + 1, i)
+            quant_pa(c)
+        for cc in range(NC):
+            load_wi(cc, 1)
+        for i in range(NT):
+            load_lg(i)
+        gu = [(2, 0), (3, 0), (0, 1), (1, 1)]
+        fin = []
+        todo2 = [(i, h) for h in range(NH) for i in range(N1)]
+        for k, i in enumerate(range(N1, NT)):
+            for c in range(NC):
+                stage1(c, i)
+            for c in range(NC):
+                square(c, i)
+            if k == 0:
+                quant_wi(0, 0)
+                quant_wi(1, 0)
+                spread_wi(2, 0, [("g", 0, N)])
+                spread_wi(3, 0, W)
+            if k == 1:
+                quant_wi(2, 0)
+                quant_wi(3, 0)
+                spread_wi(0, 1, [("s", 0, N)])
+                spread_wi(1, 1, [("g", 0, N)])
+            if k == 2:
+                quant_wi(0, 1)
+                quant_wi(1, 1)
+                spread_wi(2, 1, [("s", 0, N)])
+                spread_wi(3, 1, [("g", 0, N)])
+            if k == 3:
+                quant_wi(2, 1)
+                quant_wi(3, 1)
+            gate(0, i)
+            gate(1, i)
+            gate(2, i)
+            gate(3, i)
+            if k >= 2:
+                for _ in range(2):
+                    ih = todo2.pop(0)
+                    stage2(*ih)
+                    fin.append(ih)
+            turn([(0, i), (1, i)])
+            turn([(2, i), (3, i)])
+            empty([(0, i), (1, i)], ("b", i), 0, "s")
+            empty([(2, i), (3, i)], ("b", i), 1, "s")
+            for ih in fin:
+                finish(*ih)
+            fin = []
+            quant_pb(i)
+        todo2 = todo2 + [(i, h) for i in range(N1, NT) for h in range(NH)]
+        for ih in todo2:
+            stage2(*ih)
+            finish(*ih)

@@ -18,7 +18,40 @@ NT = T // P
 NC = F // N
 NG = D // N
 NH = D // N
-PLAN = {"wo": [("vv", "ss")] * 3, "wi": {}}
+ORDER = [
+    ("ld", "o", 0, 0), ("ld", "a", 0), ("ld", "o", 0, 1), ("ld", "u", 0), ("ld", "s"), ("ld", "o", 1, 0), ("ld", "o", 1, 1), ("ld", "o", 2, 0),
+    ("ld", "a", 1), ("co", 0, 0, 0, "v"), ("co", 0, 0, 1, "s"), ("ld", "o", 2, 1), ("qo", 0, 0), ("sq", 0, 0), ("sq", 0, 1), ("ld", "a", 3),
+    ("sq", 0, 2), ("co", 0, 1, 0, "v"), ("co", 0, 1, 1, "s"), ("ld", "a", 2), ("ld", "o", 3, 0), ("sq", 0, 3), ("qo", 0, 1), ("mm", 0, 0),
+    ("ld", "o", 3, 1), ("co", 1, 0, 0, "v"), ("co", 1, 0, 1, "s"), ("mm", 0, 1), ("ga", 0, 0), ("ld", "u", 1), ("mm", 0, 2), ("qo", 1, 0),
+    ("co", 1, 1, 0, "s"), ("mm", 0, 3), ("ga", 0, 1), ("ld", "b", 4), ("co", 1, 1, 1, "v"), ("tu", 0, 0), ("co", 2, 0, 0, "s"), ("ga", 0, 2),
+    ("ld", "i", 0, 0), ("qo", 1, 1), ("ev", 0, 0, "s"), ("ga", 0, 3), ("mm", 1, 0), ("sq", 1, 0), ("ld", "i", 1, 0), ("co", 2, 0, 1, "v"),
+    ("sq", 1, 1), ("mm", 1, 1), ("ga", 1, 0), ("sq", 1, 2), ("mm", 1, 2), ("ld", "b", 6), ("ga", 1, 1), ("co", 2, 1, 0, "s"),
+    ("tu", 0, 1), ("mm", 1, 3), ("co", 2, 1, 1, "v"), ("ev", 0, 1, "v"), ("tu", 1, 0), ("ld", "i", 3, 0), ("sq", 1, 3), ("qo", 2, 0),
+    ("ev", 1, 0, "s"), ("qp", 0), ("sq", 2, 0), ("ld", "i", 2, 0), ("qo", 2, 1), ("sq", 2, 1), ("ga", 1, 2), ("sq", 2, 2),
+    ("mm", 2, 0), ("ld", "i", 2, 1), ("ga", 1, 3), ("co", 3, 0, 0, "s"), ("co", 3, 0, 1, "v"), ("mm", 2, 1), ("ld", "b", 5), ("ga", 2, 0),
+    ("co", 3, 1, 0, "s"), ("mm", 2, 2), ("co", 3, 1, 1, "v"), ("ld", "i", 1, 1), ("tu", 1, 1), ("sq", 2, 3), ("ga", 2, 1), ("mm", 2, 3),
+    ("ev", 1, 1, "s"), ("qo", 3, 0), ("tu", 2, 0), ("ld", "i", 0, 1), ("sq", 3, 0), ("qo", 3, 1), ("mm", 0, 4), ("ev", 2, 0, "s"),
+    ("qp", 1), ("mm", 3, 0), ("sq", 3, 1), ("ga", 2, 2), ("ld", "b", 7), ("mm", 3, 1), ("sq", 3, 2), ("ga", 2, 3),
+    ("mm", 3, 2), ("sq", 3, 3), ("ga", 3, 0), ("ld", "i", 3, 1), ("tu", 2, 1), ("ci", 0, 0, 0, "s"), ("ga", 3, 1), ("mm", 3, 3),
+    ("ev", 2, 1, "v"), ("tu", 3, 0), ("ld", "l", 0), ("ci", 0, 0, 1, "s"), ("ga", 3, 2), ("mm", 1, 4), ("qp", 2), ("mm", 2, 4),
+    ("ld", "l", 1), ("ev", 3, 0, "s"), ("ga", 3, 3), ("mm", 3, 4), ("sq", 0, 4), ("qi", 0, 0), ("mm", 0, 5), ("sq", 1, 4),
+    ("ci", 1, 0, 0, "v"), ("ld", "l", 2), ("tu", 3, 1), ("ci", 1, 0, 1, "s"), ("mm", 1, 5), ("ga", 0, 4), ("mm", 2, 5), ("ld", "l", 3),
+    ("ev", 3, 1, "v"), ("sq", 2, 4), ("mm", 3, 5), ("ga", 1, 4), ("sq", 3, 4), ("mm", 0, 6), ("qi", 1, 0), ("ld", "l", 4),
+    ("ci", 2, 0, 0, "s"), ("tu", 4, 0), ("qp", 3), ("ci", 2, 0, 1, "v"), ("ld", "l", 5), ("ev", 4, 0, "s"), ("ga", 2, 4), ("sq", 0, 5),
+    ("mm", 1, 6), ("qi", 2, 0), ("ld", "l", 6), ("ci", 3, 0, 0, "s"), ("mm", 2, 6), ("ga", 3, 4), ("ci", 3, 0, 1, "v"), ("tu", 4, 1),
+    ("sq", 1, 5), ("ld", "l", 7), ("ga", 0, 5), ("ev", 4, 1, "s"), ("qi", 3, 0), ("mm", 3, 6), ("sq", 2, 5), ("ga", 1, 5),
+    ("s2", 0, 0), ("ci", 0, 1, 0, "s"), ("ci", 0, 1, 1, "v"), ("qp", 4), ("tu", 5, 0), ("sq", 3, 5), ("qi", 0, 1), ("ev", 5, 0, "s"),
+    ("ga", 2, 5), ("sq", 0, 6), ("s2", 1, 0), ("ci", 1, 1, 0, "v"), ("ci", 1, 1, 1, "s"), ("ga", 3, 5), ("s2", 2, 0), ("fi", 0, 0),
+    ("sq", 1, 6), ("qi", 1, 1), ("ci", 2, 1, 0, "s"), ("tu", 5, 1), ("ga", 0, 6), ("mm", 0, 7), ("ev", 5, 1, "v"), ("ci", 2, 1, 1, "s"),
+    ("s2", 3, 0), ("fi", 1, 0), ("ga", 1, 6), ("mm", 1, 7), ("sq", 2, 6), ("qi", 2, 1), ("tu", 6, 0), ("sq", 3, 6),
+    ("qp", 5), ("s2", 4, 0), ("ev", 6, 0, "s"), ("fi", 2, 0), ("ci", 3, 1, 0, "s"), ("ga", 2, 6), ("mm", 2, 7), ("ci", 3, 1, 1, "v"),
+    ("s2", 5, 0), ("sq", 0, 7), ("fi", 3, 0), ("sq", 1, 7), ("mm", 3, 7), ("qi", 3, 1), ("sq", 2, 7), ("ga", 3, 6),
+    ("s2", 0, 1), ("sq", 3, 7), ("fi", 4, 0), ("ga", 0, 7), ("tu", 6, 1), ("s2", 1, 1), ("fi", 5, 0), ("ev", 6, 1, "s"),
+    ("ga", 1, 7), ("qp", 6), ("s2", 2, 1), ("ga", 2, 7), ("s2", 6, 0), ("ga", 3, 7), ("fi", 0, 1), ("tu", 7, 0),
+    ("fi", 1, 1), ("tu", 7, 1), ("ev", 7, 0, "s"), ("fi", 6, 0), ("s2", 3, 1), ("ev", 7, 1, "s"), ("fi", 2, 1), ("qp", 7),
+    ("s2", 4, 1), ("fi", 3, 1), ("s2", 7, 0), ("fi", 4, 1), ("s2", 5, 1), ("fi", 7, 0), ("s2", 6, 1), ("fi", 5, 1),
+    ("s2", 7, 1), ("fi", 6, 1), ("fi", 7, 1),
+]
 N1 = 4
 
 def tile_implicit_adjoint_step_e3_kernel(tc, u_words, u_scales, w_out, act, w_in, loss_grad, out):
@@ -28,6 +61,7 @@ def tile_implicit_adjoint_step_e3_kernel(tc, u_words, u_scales, w_out, act, w_in
         raws = ctx.enter_context(tc.tile_pool(name="raws", bufs=8))
         work = ctx.enter_context(tc.tile_pool(name="work", bufs=4))
         psum = ctx.enter_context(tc.psum_pool(name="psum", bufs=8))
+        ctx.enter_context(tc.manual_schedule())
 
         u_c = keep.tile([P, NG, T], U32, name="u_c", align_bytes=64)
         u_s = keep.tile([P, NG, T], U8, name="u_s", align_bytes=64)
@@ -53,7 +87,7 @@ def tile_implicit_adjoint_step_e3_kernel(tc, u_words, u_scales, w_out, act, w_in
         wo_raw, act1, act2, wi_raw, lg = {}, {}, {}, {}, {}
 
         def load_wo(c, g):
-            t = raws.tile([P, 4, N], BF16, name="raw", bufs=12, align_bytes=64)
+            t = raws.tile([P, 4, N], BF16, name="raw", bufs=10, align_bytes=64)
             nc.sync.dma_start(out=t[:], in_=wo_v[g, :, :, c * N:(c + 1) * N])
             wo_raw[c, g] = t
 
@@ -68,7 +102,7 @@ def tile_implicit_adjoint_step_e3_kernel(tc, u_words, u_scales, w_out, act, w_in
             act2[i] = t
 
         def load_wi(c, h):
-            t = raws.tile([P, 4, N], BF16, name="raw", bufs=12, align_bytes=64)
+            t = raws.tile([P, 4, N], BF16, name="raw", bufs=10, align_bytes=64)
             nc.sync.dma_start(out=t[:], in_=wi_v[c, :, :, h * N:(h + 1) * N])
             wi_raw[c, h] = t
 
@@ -78,13 +112,14 @@ def tile_implicit_adjoint_step_e3_kernel(tc, u_words, u_scales, w_out, act, w_in
             lg[i] = t
 
         grouped = {}
+        ready = set()
 
-        def spread_wo(c, g, engs):
+        def spread_wo(c, g, u, e):
             raw = wo_raw[c, g]
             if ("o", c, g) not in grouped:
                 grouped["o", c, g] = work.tile([P, N, 4], BF16, name="grouped", bufs=5, align_bytes=64)
             dst = grouped["o", c, g]
-            for u, e in enumerate(engs):
+            if True:
                 o = dst[:, u * 256:(u + 1) * 256, :].rearrange("p (q e) t -> p q t e", e=2)
                 s = raw[:].rearrange("p t (q u e) -> p u q t e", u=2, e=2)[:, u]
                 if e == "v":
@@ -109,9 +144,11 @@ def tile_implicit_adjoint_step_e3_kernel(tc, u_words, u_scales, w_out, act, w_in
                     nc.gpsimd.tensor_scalar(out=dst[:, a:b, :], in0=raw[:, :, a:b].rearrange("p t c -> p c t"), scalar1=1.0, scalar2=0.0, op0=ALU.mult, op1=ALU.add)
 
         def quant_wo(c, g):
+            ready.add(("o", c, g))
             nc.vector.quantize_mx(out=wo_c[:, c, g, :].bitcast(E4X4), scales=wo_s[:, c, g, :], in_=grouped.pop(("o", c, g))[:].rearrange("p c t -> p (c t)"))
 
         def quant_wi(c, h):
+            ready.add((c, h))
             nc.vector.quantize_mx(out=wi_c[:, h, c, :].bitcast(E4X4), scales=wi_s[:, h, c, :], in_=grouped.pop(("i", c, h))[:].rearrange("p c t -> p (c t)"))
 
         def spread_wi(c, h, parts):
@@ -123,6 +160,7 @@ def tile_implicit_adjoint_step_e3_kernel(tc, u_words, u_scales, w_out, act, w_in
             if (c, i) not in back:
                 back[c, i] = psum.tile([P, N], F32, name="bank")
             for g in gs:
+                assert ("o", c, g) in ready
                 nc.tensor.matmul_mx(out=back[c, i][:], lhsT=u_c[:, g, i * P:(i + 1) * P].bitcast(E5X4), lhsT_scale=u_s[:, g, i * P:(i + 1) * P],
                                     rhs=wo_c[:, c, g, :].bitcast(E4X4), rhs_scale=wo_s[:, c, g, :], start=(g == 0), stop=(g == NG - 1))
 
@@ -170,119 +208,65 @@ def tile_implicit_adjoint_step_e3_kernel(tc, u_words, u_scales, w_out, act, w_in
                     l, s = pa_c[:, c, i * P:(i + 1) * P], pa_s[:, c, i * P:(i + 1) * P]
                 else:
                     l, s = pb_c[:, i - N1, c, :], pb_s[:, i - N1, c, :]
+                assert (c, h) in ready
                 nc.tensor.matmul_mx(out=t[:], lhsT=l.bitcast(E5X4), lhsT_scale=s, rhs=wi_c[:, h, c, :].bitcast(E4X4), rhs_scale=wi_s[:, h, c, :], start=(c == 0), stop=(c == NC - 1))
             vjp[i, h] = t
 
         def finish(i, h):
-            t = work.tile([P, N], F32, name="res", bufs=4)
+            t = work.tile([P, N], F32, name="res", bufs=6)
             nc.vector.tensor_tensor(out=t[:], in0=lg[i][:, h * N:(h + 1) * N], in1=vjp.pop((i, h))[:], op=ALU.subtract)
             nc.sync.dma_start(out=out_v[i, :, h * N:(h + 1) * N], in_=t[:])
 
         uw = u_words.rearrange("g p n t -> p g (n t)")
-        def load_u(g):
-            nc.sync.dma_start(out=u_c[:, g, :].bitcast(I32), in_=uw[:, g, :].bitcast(I32))
-        load_wo(0, 0)
-        load_wo(0, 1)
-        for q in range(4):
-            nc.sync.dma_start(out=u_s[32 * q:32 * q + 4, :, :].bitcast(I32), in_=u_scales[:, 4 * q:4 * q + 4, :].rearrange("g q n -> q g n").bitcast(I32))
-        load_u(0)
-        load_act1(0)
-        load_u(1)
-        for c in range(1, NC):
-            load_wo(c, 0)
-            load_wo(c, 1)
-            load_act1(c)
-        load_wi(0, 0)
-        load_act2(4)
-        load_wi(1, 0)
-        load_wi(2, 0)
-        load_act2(5)
-        load_wi(3, 0)
-        load_act2(6)
-        load_act2(7)
 
-        W = [("v", 0, N)]
-        spread_wo(0, 0, "vs")
-        spread_wo(0, 1, "vs")
-        quant_wo(0, 0)
-        quant_wo(0, 1)
-        for i in range(N1):
-            stage1(0, i, (0,))
-        for i in range(N1):
-            stage1(0, i, (1,))
-        for i in range(N1):
-            square(0, i)
-        for c in range(NC):
-            if c + 1 < NC:
-                spread_wo(c + 1, 0, PLAN["wo"][c][0])
-                spread_wo(c + 1, 1, PLAN["wo"][c][1])
-                quant_wo(c + 1, 0)
+        def load_u(b):
+            w = T // 2
+            nc.sync.dma_start(out=u_c[:, :, b * w:(b + 1) * w].bitcast(I32), in_=uw[:, :, 4 * b * w:4 * (b + 1) * w].bitcast(I32))
+
+        def load_s():
+            for q in range(4):
+                nc.sync.dma_start(out=u_s[32 * q:32 * q + 4, :, :].bitcast(I32), in_=u_scales[:, 4 * q:4 * q + 4, :].rearrange("g q n -> q g n").bitcast(I32))
+
+        loaders = {"o": load_wo, "a": load_act1, "s": load_s, "u": load_u, "b": load_act2, "i": load_wi, "l": load_lg}
+
+        def cells(s):
+            return [(s, i) for i in range(N1)] if s < NC else [(c, s - NC + N1) for c in range(NC)]
+
+        def quant_p(s):
+            if s < NC:
+                quant_pa(s)
             else:
-                spread_wi(0, 0, [("g", 0, N)])
-                spread_wi(1, 0, [("g", 0, N)])
-            gate(c, 0)
-            gate(c, 1)
-            turn([(c, 0), (c, 1)])
-            empty([(c, 0), (c, 1)], ("a", c), 0, "s")
-            gate(c, 2)
-            gate(c, 3)
-            turn([(c, 2), (c, 3)])
-            empty([(c, 2), (c, 3)], ("a", c), 1, "s")
-            if c + 1 < NC:
-                quant_wo(c + 1, 1)
-                for i in range(N1):
-                    stage1(c + 1, i)
-                for i in range(N1):
-                    square(c + 1, i)
-            quant_pa(c)
-        for cc in range(NC):
-            load_wi(cc, 1)
-        for i in range(NT):
-            load_lg(i)
-        gu = [(2, 0), (3, 0), (0, 1), (1, 1)]
-        fin = []
-        todo2 = [(i, h) for h in range(NH) for i in range(N1)]
-        for k, i in enumerate(range(N1, NT)):
-            for c in range(NC):
-                stage1(c, i)
-            for c in range(NC):
-                square(c, i)
-            if k == 0:
-                quant_wi(0, 0)
-                quant_wi(1, 0)
-                spread_wi(2, 0, [("g", 0, N)])
-                spread_wi(3, 0, W)
-            if k == 1:
-                quant_wi(2, 0)
-                quant_wi(3, 0)
-                spread_wi(0, 1, [("s", 0, N)])
-                spread_wi(1, 1, [("g", 0, N)])
-            if k == 2:
-                quant_wi(0, 1)
-                quant_wi(1, 1)
-                spread_wi(2, 1, [("s", 0, N)])
-                spread_wi(3, 1, [("g", 0, N)])
-            if k == 3:
-                quant_wi(2, 1)
-                quant_wi(3, 1)
-            gate(0, i)
-            gate(1, i)
-            gate(2, i)
-            gate(3, i)
-            if k >= 2:
-                for _ in range(2):
-                    ih = todo2.pop(0)
-                    stage2(*ih)
-                    fin.append(ih)
-            turn([(0, i), (1, i)])
-            turn([(2, i), (3, i)])
-            empty([(0, i), (1, i)], ("b", i), 0, "s")
-            empty([(2, i), (3, i)], ("b", i), 1, "s")
-            for ih in fin:
-                finish(*ih)
-            fin = []
-            quant_pb(i)
-        todo2 = todo2 + [(i, h) for i in range(N1, NT) for h in range(NH)]
-        for ih in todo2:
-            stage2(*ih)
-            finish(*ih)
+                quant_pb(s - NC + N1)
+
+        def key(s):
+            return ("a", s) if s < NC else ("b", s - NC + N1)
+
+        for word in ORDER:
+            w = word
+            a = w[1:]
+            if w[0] == "ld":
+                loaders[w[1]](*w[2:])
+            elif w[0] == "co":
+                spread_wo(a[0], a[1], a[2], w[4])
+            elif w[0] == "ci":
+                spread_wi(a[0], a[1], [(w[4], 256 * a[2], 256 * a[2] + 256)])
+            elif w[0] == "qo":
+                quant_wo(*a)
+            elif w[0] == "qi":
+                quant_wi(*a)
+            elif w[0] == "sq":
+                square(*a)
+            elif w[0] == "mm":
+                stage1(*a)
+            elif w[0] == "ga":
+                gate(*a)
+            elif w[0] == "tu":
+                turn(cells(a[0])[2 * a[1]:2 * a[1] + 2])
+            elif w[0] == "ev":
+                empty(cells(a[0])[2 * a[1]:2 * a[1] + 2], key(a[0]), a[1], w[3])
+            elif w[0] == "qp":
+                quant_p(a[0])
+            elif w[0] == "s2":
+                stage2(*a)
+            elif w[0] == "fi":
+                finish(*a)

from contextlib import ExitStack
import concourse.mybir as mybir
from concourse.masks import make_identity
F32 = mybir.dt.float32
BF16 = mybir.dt.bfloat16
U32 = mybir.dt.uint32
I32 = mybir.dt.int32
U8 = mybir.dt.uint8
E4X4 = mybir.dt.float8_e4m3fn_x4
E5X4 = mybir.dt.float8_e5m2_x4
ALU = mybir.AluOpType
ACT = mybir.ActivationFunctionType
T, D, F = 1024, 1024, 2048
FLOPS = 2 * 2 * T * D * F
P = 128
N = 512
NT = T // P
NC = F // N
NG = D // N
NH = D // N
ORDER = [
    ("ld", "o", 0, 0), ("ld", "a", 0), ("ld", "o", 0, 1), ("ld", "u", 0), ("ld", "s"), ("ld", "o", 1, 0), ("ld", "o", 1, 1), ("ld", "o", 2, 0),
    ("ld", "a", 1), ("co", 0, 0, 0, "v"), ("co", 0, 0, 1, "s"), ("ld", "o", 2, 1), ("qo", 0, 0), ("sq", 0, 0), ("sq", 0, 1), ("ld", "a", 3),
    ("sq", 0, 2), ("co", 0, 1, 0, "v"), ("co", 0, 1, 1, "s"), ("ld", "a", 2), ("ld", "o", 3, 0), ("sq", 0, 3), ("qo", 0, 1), ("mm", 0, 0),
    ("ld", "o", 3, 1), ("co", 1, 0, 0, "v"), ("co", 1, 0, 1, "s"), ("mm", 0, 1), ("ga", 0, 0), ("ld", "u", 1), ("mm", 0, 2), ("qo", 1, 0),
    ("co", 1, 1, 0, "s"), ("mm", 0, 3), ("ga", 0, 1), ("ld", "b", 4), ("co", 1, 1, 1, "v"), ("tu", 0, 0), ("co", 2, 0, 0, "s"), ("ga", 0, 2),
    ("ld", "i", 0, 0), ("qo", 1, 1), ("ev", 0, 0, "s"), ("ga", 0, 3), ("mm", 1, 0), ("sq", 1, 0), ("ld", "i", 1, 0), ("co", 2, 0, 1, "v"),
    ("sq", 1, 1), ("mm", 1, 1), ("ga", 1, 0), ("sq", 1, 2), ("mm", 1, 2), ("ld", "b", 6), ("ga", 1, 1), ("co", 2, 1, 0, "s"),
    ("tu", 0, 1), ("mm", 1, 3), ("co", 2, 1, 1, "v"), ("ev", 0, 1, "v"), ("tu", 1, 0), ("ld", "i", 3, 0), ("sq", 1, 3), ("qo", 2, 0),
    ("ev", 1, 0, "s"), ("qp", 0), ("sq", 2, 0), ("ld", "i", 2, 0), ("qo", 2, 1), ("sq", 2, 1), ("ga", 1, 2), ("sq", 2, 2),
    ("mm", 2, 0), ("ld", "i", 2, 1), ("ga", 1, 3), ("co", 3, 0, 0, "s"), ("co", 3, 0, 1, "v"), ("mm", 2, 1), ("ld", "b", 5), ("ga", 2, 0),
    ("co", 3, 1, 0, "s"), ("mm", 2, 2), ("co", 3, 1, 1, "v"), ("ld", "i", 1, 1), ("tu", 1, 1), ("sq", 2, 3), ("ga", 2, 1), ("mm", 2, 3),
    ("ev", 1, 1, "s"), ("qo", 3, 0), ("tu", 2, 0), ("ld", "i", 0, 1), ("sq", 3, 0), ("qo", 3, 1), ("mm", 0, 4), ("ev", 2, 0, "s"),
    ("qp", 1), ("mm", 3, 0), ("sq", 3, 1), ("ga", 2, 2), ("ld", "b", 7), ("mm", 3, 1), ("sq", 3, 2), ("ga", 2, 3),
    ("mm", 3, 2), ("sq", 3, 3), ("ga", 3, 0), ("ld", "i", 3, 1), ("tu", 2, 1), ("ci", 0, 0, 0, "s"), ("ga", 3, 1), ("mm", 3, 3),
    ("ev", 2, 1, "v"), ("tu", 3, 0), ("ld", "l", 0), ("ci", 0, 0, 1, "s"), ("ga", 3, 2), ("mm", 1, 4), ("qp", 2), ("mm", 2, 4),
    ("ld", "l", 1), ("ev", 3, 0, "s"), ("ga", 3, 3), ("mm", 3, 4), ("sq", 0, 4), ("qi", 0, 0), ("mm", 0, 5), ("sq", 1, 4),
    ("ci", 1, 0, 0, "v"), ("ld", "l", 2), ("tu", 3, 1), ("ci", 1, 0, 1, "s"), ("mm", 1, 5), ("ga", 0, 4), ("mm", 2, 5), ("ld", "l", 3),
    ("ev", 3, 1, "v"), ("sq", 2, 4), ("mm", 3, 5), ("ga", 1, 4), ("sq", 3, 4), ("mm", 0, 6), ("qi", 1, 0), ("ld", "l", 4),
    ("ci", 2, 0, 0, "s"), ("tu", 4, 0), ("qp", 3), ("ci", 2, 0, 1, "v"), ("ld", "l", 5), ("ev", 4, 0, "s"), ("ga", 2, 4), ("sq", 0, 5),
    ("mm", 1, 6), ("qi", 2, 0), ("ld", "l", 6), ("ci", 3, 0, 0, "s"), ("mm", 2, 6), ("ga", 3, 4), ("ci", 3, 0, 1, "v"), ("tu", 4, 1),
    ("sq", 1, 5), ("ld", "l", 7), ("ga", 0, 5), ("ev", 4, 1, "s"), ("qi", 3, 0), ("mm", 3, 6), ("sq", 2, 5), ("ga", 1, 5),
    ("s2", 0, 0), ("ci", 0, 1, 0, "s"), ("ci", 0, 1, 1, "v"), ("qp", 4), ("tu", 5, 0), ("sq", 3, 5), ("qi", 0, 1), ("ev", 5, 0, "s"),
    ("ga", 2, 5), ("sq", 0, 6), ("s2", 1, 0), ("ci", 1, 1, 0, "v"), ("ci", 1, 1, 1, "s"), ("ga", 3, 5), ("s2", 2, 0), ("fi", 0, 0),
    ("sq", 1, 6), ("qi", 1, 1), ("ci", 2, 1, 0, "s"), ("tu", 5, 1), ("ga", 0, 6), ("mm", 0, 7), ("ev", 5, 1, "v"), ("ci", 2, 1, 1, "s"),
    ("s2", 3, 0), ("fi", 1, 0), ("ga", 1, 6), ("mm", 1, 7), ("sq", 2, 6), ("qi", 2, 1), ("tu", 6, 0), ("sq", 3, 6),
    ("qp", 5), ("s2", 4, 0), ("ev", 6, 0, "s"), ("fi", 2, 0), ("ci", 3, 1, 0, "s"), ("ga", 2, 6), ("mm", 2, 7), ("ci", 3, 1, 1, "v"),
    ("s2", 5, 0), ("sq", 0, 7), ("fi", 3, 0), ("sq", 1, 7), ("mm", 3, 7), ("qi", 3, 1), ("sq", 2, 7), ("ga", 3, 6),
    ("s2", 0, 1), ("sq", 3, 7), ("fi", 4, 0), ("ga", 0, 7), ("tu", 6, 1), ("s2", 1, 1), ("fi", 5, 0), ("ev", 6, 1, "s"),
    ("ga", 1, 7), ("qp", 6), ("s2", 2, 1), ("ga", 2, 7), ("s2", 6, 0), ("ga", 3, 7), ("fi", 0, 1), ("tu", 7, 0),
    ("fi", 1, 1), ("tu", 7, 1), ("ev", 7, 0, "s"), ("fi", 6, 0), ("s2", 3, 1), ("ev", 7, 1, "s"), ("fi", 2, 1), ("qp", 7),
    ("s2", 4, 1), ("fi", 3, 1), ("s2", 7, 0), ("fi", 4, 1), ("s2", 5, 1), ("fi", 7, 0), ("s2", 6, 1), ("fi", 5, 1),
    ("s2", 7, 1), ("fi", 6, 1), ("fi", 7, 1),
]
N1 = 4

def tile_implicit_adjoint_step_e3_kernel(tc, u_words, u_scales, w_out, act, w_in, loss_grad, out):
    nc = tc.nc
    with ExitStack() as ctx:
        keep = ctx.enter_context(tc.tile_pool(name="keep", bufs=1))
        raws = ctx.enter_context(tc.tile_pool(name="raws", bufs=8))
        work = ctx.enter_context(tc.tile_pool(name="work", bufs=4))
        psum = ctx.enter_context(tc.psum_pool(name="psum", bufs=8))
        ctx.enter_context(tc.manual_schedule())

        u_c = keep.tile([P, NG, T], U32, name="u_c", align_bytes=64)
        u_s = keep.tile([P, NG, T], U8, name="u_s", align_bytes=64)
        wo_c = keep.tile([P, NC, NG, N], U32, name="wo_c", align_bytes=64)
        wo_s = keep.tile([P, NC, NG, N], U8, name="wo_s", align_bytes=64)
        wi_c = keep.tile([P, NH, NC, N], U32, name="wi_c", align_bytes=64)
        wi_s = keep.tile([P, NH, NC, N], U8, name="wi_s", align_bytes=64)
        pa_c = keep.tile([P, NC, N1 * P], U32, name="pa_c", align_bytes=64)
        pa_s = keep.tile([P, NC, N1 * P], U8, name="pa_s", align_bytes=64)
        pb_c = keep.tile([P, NT - N1, NC, P], U32, name="pb_c", align_bytes=64)
        pb_s = keep.tile([P, NT - N1, NC, P], U8, name="pb_s", align_bytes=64)
        ident = keep.tile([P, P], F32, name="ident", align_bytes=64)

        nc.gpsimd.memset(u_s[:].rearrange("p g n -> p (g n)").bitcast(I32), 0)
        make_identity(nc, ident[:])

        wo_v = w_out.rearrange("(g p j) f -> g p j f", p=P, j=4)
        wi_v = w_in.rearrange("(c p j) d -> c p j d", p=P, j=4)
        act_v = act.rearrange("(i p) f -> p i f", p=P)
        lg_v = loss_grad.rearrange("(i p) d -> i p d", p=P)
        out_v = out.rearrange("(i p) d -> i p d", p=P)

        wo_raw, act1, act2, wi_raw, lg = {}, {}, {}, {}, {}

        def load_wo(c, g):
            t = raws.tile([P, 4, N], BF16, name="raw", bufs=10, align_bytes=64)
            nc.sync.dma_start(out=t[:], in_=wo_v[g, :, :, c * N:(c + 1) * N])
            wo_raw[c, g] = t

        def load_act1(c):
            t = raws.tile([P, N1, N], BF16, name="act1", bufs=4)
            nc.sync.dma_start(out=t[:], in_=act_v[:, 0:N1, c * N:(c + 1) * N])
            act1[c] = t

        def load_act2(i):
            t = raws.tile([P, F], BF16, name="act2", bufs=4)
            nc.sync.dma_start(out=t[:], in_=act_v[:, i, :])
            act2[i] = t

        def load_wi(c, h):
            t = raws.tile([P, 4, N], BF16, name="raw", bufs=10, align_bytes=64)
            nc.sync.dma_start(out=t[:], in_=wi_v[c, :, :, h * N:(h + 1) * N])
            wi_raw[c, h] = t

        def load_lg(i):
            t = raws.tile([P, D], BF16, name="lg", bufs=8)
            nc.sync.dma_start(out=t[:], in_=lg_v[i])
            lg[i] = t

        grouped = {}
        ready = set()

        def spread_wo(c, g, u, e):
            raw = wo_raw[c, g]
            if ("o", c, g) not in grouped:
                grouped["o", c, g] = work.tile([P, N, 4], BF16, name="grouped", bufs=5, align_bytes=64)
            dst = grouped["o", c, g]
            if True:
                o = dst[:, u * 256:(u + 1) * 256, :].rearrange("p (q e) t -> p q t e", e=2)
                s = raw[:].rearrange("p t (q u e) -> p u q t e", u=2, e=2)[:, u]
                if e == "v":
                    nc.vector.tensor_copy(out=o, in_=s)
                elif e == "s":
                    nc.scalar.copy(out=o, in_=s)
                elif e == "g":
                    nc.gpsimd.tensor_scalar(out=dst[:, u * 256:(u + 1) * 256, :].rearrange("p (q e) t -> p q e t", e=2), in0=raw[:].rearrange("p t (q u e) -> p u q e t", u=2, e=2)[:, u], scalar1=1.0, scalar2=0.0, op0=ALU.mult, op1=ALU.add)

        def spread(raw, key, parts):
            if key not in grouped:
                grouped[key] = work.tile([P, N, 4], BF16, name="grouped", bufs=5, align_bytes=64)
            dst = grouped[key]
            for e, a, b in parts:
                o = dst[:, a:b, :].rearrange("p (c i) t -> p c t i", i=4)
                s = raw[:, :, a:b].rearrange("p t (c i) -> p c t i", i=4)
                if e == "v":
                    nc.vector.tensor_copy(out=o, in_=s)
                elif e == "s":
                    nc.scalar.copy(out=o, in_=s)
                else:
                    nc.gpsimd.tensor_scalar(out=dst[:, a:b, :], in0=raw[:, :, a:b].rearrange("p t c -> p c t"), scalar1=1.0, scalar2=0.0, op0=ALU.mult, op1=ALU.add)

        def quant_wo(c, g):
            ready.add(("o", c, g))
            nc.vector.quantize_mx(out=wo_c[:, c, g, :].bitcast(E4X4), scales=wo_s[:, c, g, :], in_=grouped.pop(("o", c, g))[:].rearrange("p c t -> p (c t)"))

        def quant_wi(c, h):
            ready.add((c, h))
            nc.vector.quantize_mx(out=wi_c[:, h, c, :].bitcast(E4X4), scales=wi_s[:, h, c, :], in_=grouped.pop(("i", c, h))[:].rearrange("p c t -> p (c t)"))

        def spread_wi(c, h, parts):
            spread(wi_raw[c, h], ("i", c, h), parts)

        back, sq, pre, turned, gpre = {}, {}, {}, {}, {}

        def stage1(c, i, gs=(0, 1)):
            if (c, i) not in back:
                back[c, i] = psum.tile([P, N], F32, name="bank")
            for g in gs:
                assert ("o", c, g) in ready
                nc.tensor.matmul_mx(out=back[c, i][:], lhsT=u_c[:, g, i * P:(i + 1) * P].bitcast(E5X4), lhsT_scale=u_s[:, g, i * P:(i + 1) * P],
                                    rhs=wo_c[:, c, g, :].bitcast(E4X4), rhs_scale=wo_s[:, c, g, :], start=(g == 0), stop=(g == NG - 1))

        def square(c, i):
            t = work.tile([P, N], F32, name="sq", bufs=8)
            src = act1[c][:, i, :] if i < N1 else act2[i][:, c * N:(c + 1) * N]
            nc.scalar.activation(out=t[:].rearrange("q (u p e) -> q u p e", u=2, e=2), in_=src.rearrange("q (p u e) -> q u p e", u=2, e=2), func=ACT.Square)
            sq[c, i] = t

        def gate(c, i):
            t = work.tile([P, N], BF16, name="pre", bufs=8)
            nc.vector.scalar_tensor_tensor(out=t[:], in0=sq.pop((c, i))[:], scalar=1.0, in1=back.pop((c, i))[:], op0=ALU.subtract, op1=ALU.mult)
            pre[c, i] = t

        def turn(pairs):
            t = psum.tile([P, 2, 2, P], F32, name="bank")
            for k, ci in enumerate(pairs):
                w = pre.pop(ci)[:].bitcast(F32)
                for u in (0, 1):
                    nc.tensor.transpose(out=t[:, k, u, :], in_=w[:, u * P:(u + 1) * P], identity=ident[:])
            turned[pairs[0]] = t

        def empty(pairs, key, slot, eng):
            if key not in gpre:
                gpre[key] = work.tile([P, 4 * P, 4], BF16, name="gpre", bufs=3, align_bytes=64)
            dst = gpre[key][:, slot * 256:(slot + 1) * 256, :].rearrange("p r t -> p (r t)").bitcast(F32).rearrange("p (k r u) -> p k r u", k=2, u=2)
            src = turned.pop(pairs[0])[:].rearrange("p k u r -> p k r u")
            if eng == "s":
                nc.scalar.copy(out=dst, in_=src)
            else:
                nc.vector.tensor_copy(out=dst, in_=src)

        def quant_pa(c):
            nc.vector.quantize_mx(out=pa_c[:, c, :].bitcast(E5X4), scales=pa_s[:, c, :], in_=gpre.pop(("a", c))[:].rearrange("p r t -> p (r t)"))

        def quant_pb(i):
            nc.vector.quantize_mx(out=pb_c[:, i - N1].rearrange("p c r -> p (c r)").bitcast(E5X4), scales=pb_s[:, i - N1].rearrange("p c r -> p (c r)"), in_=gpre.pop(("b", i))[:].rearrange("p r t -> p (r t)"))

        vjp = {}

        def stage2(i, h):
            t = psum.tile([P, N], F32, name="bank")
            for c in range(NC):
                if i < N1:
                    l, s = pa_c[:, c, i * P:(i + 1) * P], pa_s[:, c, i * P:(i + 1) * P]
                else:
                    l, s = pb_c[:, i - N1, c, :], pb_s[:, i - N1, c, :]
                assert (c, h) in ready
                nc.tensor.matmul_mx(out=t[:], lhsT=l.bitcast(E5X4), lhsT_scale=s, rhs=wi_c[:, h, c, :].bitcast(E4X4), rhs_scale=wi_s[:, h, c, :], start=(c == 0), stop=(c == NC - 1))
            vjp[i, h] = t

        def finish(i, h):
            t = work.tile([P, N], F32, name="res", bufs=6)
            nc.vector.tensor_tensor(out=t[:], in0=lg[i][:, h * N:(h + 1) * N], in1=vjp.pop((i, h))[:], op=ALU.subtract)
            nc.sync.dma_start(out=out_v[i, :, h * N:(h + 1) * N], in_=t[:])

        uw = u_words.rearrange("g p n t -> p g (n t)")

        def load_u(b):
            w = T // 2
            nc.sync.dma_start(out=u_c[:, :, b * w:(b + 1) * w].bitcast(I32), in_=uw[:, :, 4 * b * w:4 * (b + 1) * w].bitcast(I32))

        def load_s():
            for q in range(4):
                nc.sync.dma_start(out=u_s[32 * q:32 * q + 4, :, :].bitcast(I32), in_=u_scales[:, 4 * q:4 * q + 4, :].rearrange("g q n -> q g n").bitcast(I32))

        loaders = {"o": load_wo, "a": load_act1, "s": load_s, "u": load_u, "b": load_act2, "i": load_wi, "l": load_lg}

        def cells(s):
            return [(s, i) for i in range(N1)] if s < NC else [(c, s - NC + N1) for c in range(NC)]

        def quant_p(s):
            if s < NC:
                quant_pa(s)
            else:
                quant_pb(s - NC + N1)

        def key(s):
            return ("a", s) if s < NC else ("b", s - NC + N1)

        for word in ORDER:
            w = word
            a = w[1:]
            if w[0] == "ld":
                loaders[w[1]](*w[2:])
            elif w[0] == "co":
                spread_wo(a[0], a[1], a[2], w[4])
            elif w[0] == "ci":
                spread_wi(a[0], a[1], [(w[4], 256 * a[2], 256 * a[2] + 256)])
            elif w[0] == "qo":
                quant_wo(*a)
            elif w[0] == "qi":
                quant_wi(*a)
            elif w[0] == "sq":
                square(*a)
            elif w[0] == "mm":
                stage1(*a)
            elif w[0] == "ga":
                gate(*a)
            elif w[0] == "tu":
                turn(cells(a[0])[2 * a[1]:2 * a[1] + 2])
            elif w[0] == "ev":
                empty(cells(a[0])[2 * a[1]:2 * a[1] + 2], key(a[0]), a[1], w[3])
            elif w[0] == "qp":
                quant_p(a[0])
            elif w[0] == "s2":
                stage2(*a)
            elif w[0] == "fi":
                finish(*a)
